import numpy as np
import ml_dtypes


def mxq(x, axis, fmt="e4m3"):
    dtype, down = {"e4m3": (ml_dtypes.float8_e4m3fn, 7), "e5m2": (ml_dtypes.float8_e5m2, 14)}[fmt]
    v = np.moveaxis(np.asarray(x, np.float32).astype(ml_dtypes.bfloat16).astype(np.float64), axis, -1)
    blocks = v.reshape(v.shape[:-1] + (-1, 32))
    amax = np.abs(blocks).max(-1, keepdims=True)
    byte = np.maximum(np.where(amax > 0, np.frexp(amax)[1] - 1 + 127, 0) - down, 1)
    scale = np.exp2(byte - 127.0)
    codes = (blocks / scale).astype(np.float32).astype(dtype).astype(np.float64)
    return np.moveaxis((codes * scale).reshape(v.shape), -1, axis)


WIDE = False


def mx_kscale(k):
    if not WIDE:
        return np.ones(k)
    levels = np.array([10, -10, 5, -5, 0])
    if k % 512:
        return np.exp2(np.random.permutation(np.resize(levels, k // 32))).repeat(32)
    a = np.empty((k // 512, 16))
    for p in range(k // 512):
        a[p, :8] = np.random.permutation(np.resize(levels, 8))
        for g in range(8):
            far = levels[np.abs(levels - a[p, g]) >= 10]
            a[p, g + 8] = far[np.random.randint(len(far))]
    return np.exp2(a.ravel()).repeat(32)


def f64(x):
    return np.asarray(x).astype(np.float64)


def striped(idx):
    return np.tile(idx.reshape(-1, 16).T, (8, 1)).astype(np.uint16)


def unstriped(offs):
    return offs[:16].T.reshape(-1).astype(np.int64)


def striped8(idx):
    return np.concatenate([x.reshape(-1, 16).T for x in idx]).astype(np.uint16)


def runs(offs, k):
    lists = np.stack([offs[16 * r : 16 * r + 16].T.reshape(-1) for r in range(8)]).astype(np.int64)
    return lists[np.arange(k) % 512 // 64]


def pack_weight(w):
    k, n = w.shape
    w = f64(np.asarray(w, np.float32).astype(ml_dtypes.bfloat16)).reshape(k // 32, 32, n)
    amax = np.abs(w).max(1)
    byte = np.clip(np.where(amax > 0, np.frexp(amax)[1] - 1 + 127 - 7, 1), 1, 254)
    scaled = (w * np.exp2(127.0 - byte)[:, None, :]).reshape(k, n).astype(np.float32)
    words = np.ascontiguousarray(scaled.reshape(k // 512, 128, 4, n).transpose(0, 1, 3, 2)).astype(ml_dtypes.float8_e4m3fn).view(np.uint8)
    return words, np.ascontiguousarray(byte.astype(np.uint8).reshape(k // 512, 16, n))


def unpack_weight(words, scales):
    g, p, n, _ = words.shape
    vals = np.ascontiguousarray(words).view(ml_dtypes.float8_e4m3fn).astype(np.float64) * np.repeat(np.exp2(scales.astype(np.float64) - 127.0), 8, axis=1)[..., None]
    return vals.transpose(0, 1, 3, 2).reshape(g * 512, n)


E2M1 = np.array([0.0, 0.5, 1.0, 1.5, 2.0, 3.0, 4.0, 6.0, -0.0, -0.5, -1.0, -1.5, -2.0, -3.0, -4.0, -6.0])


def pack_fp4(w):
    k, n = w.shape
    w = f64(np.asarray(w, np.float32).astype(ml_dtypes.bfloat16)).reshape(k // 32, 32, n)
    amax = np.abs(w).max(1)
    mant, ex = np.frexp(amax / 6.0)
    byte = np.clip(np.where(amax > 0, np.where(mant > 0.5, ex, ex - 1) + 127, 1), 1, 254)
    scaled = (w * np.exp2(127.0 - byte)[:, None, :]).reshape(k, n).astype(np.float32)
    c = np.ascontiguousarray(scaled.reshape(k // 512, 128, 4, n).transpose(0, 1, 3, 2)).astype(ml_dtypes.float4_e2m1fn).view(np.uint8) & 0xF
    words = (c[..., 0::2] | (c[..., 1::2] << 4)).reshape(k // 512, 128, 2 * n)
    return np.ascontiguousarray(words), np.ascontiguousarray(byte.astype(np.uint8).reshape(k // 512, 16, n))


def unpack_fp4(words, scales):
    g, _, n = scales.shape
    words = np.ascontiguousarray(words).reshape(g, 128, n, 2)
    nib = np.empty((g, 128, n, 4), np.uint8)
    nib[..., 0::2] = words & 0xF
    nib[..., 1::2] = words >> 4
    vals = E2M1[nib] * np.repeat(np.exp2(scales.astype(np.float64) - 127.0), 8, axis=1)[..., None]
    return vals.transpose(0, 1, 3, 2).reshape(g * 512, n)


def planes(y):
    n, m = y.shape
    v = y.astype(np.float32).astype(ml_dtypes.bfloat16).astype(np.float64).reshape(n // 32, 32, m)
    top = np.abs(v).max(1)
    byte = np.clip(np.where(top > 0, np.frexp(top)[1] - 1 + 127 - 7, 1), 1, 254)
    codes = (v * np.exp2(127.0 - byte)[:, None, :]).reshape(n, m).astype(np.float32).astype(ml_dtypes.float8_e4m3fn).view(np.uint8)
    words = codes.reshape(n // 512, 128, 4, m).transpose(0, 1, 3, 2)
    return np.ascontiguousarray(words), np.ascontiguousarray(byte.astype(np.uint8).reshape(n // 512, 16, m))


K, T, S, V, G, H, U = 512, 1024, 512, 512, 2048, 512, 1024


def setup_inputs():
    n = np.random.standard_normal
    s = mx_kscale(K)[:, None]
    u = mx_kscale(S)
    packed_xT = pack_weight(n((K, T)) * s)
    packed_dT = pack_weight(n((K, G)) / s)
    packed_w1 = pack_fp4(n((K, H)) / np.sqrt(K) / s)
    return {
        "x_words": packed_xT[0],
        "x_scales": packed_xT[1],
        "d_words": packed_dT[0],
        "d_scales": packed_dT[1],
        "w1_words": packed_w1[0],
        "w1_scales": packed_w1[1],
        "mem": n((H, U)).astype(np.float32),
        "ga": (np.random.uniform(0.5, 1.5, (H, 1)) * u[:, None]).astype(np.float32),
        "gb": (np.random.uniform(0.5, 1.5, (H, 1)) / u[:, None]).astype(np.float32),
        "offs": striped(np.random.permutation(T)[:S]),
        "k1": striped8(np.random.randint(0, G, (8, H))),
        "two": striped(np.random.permutation(T)[:V]),
        "n1": striped8(np.stack([np.random.permutation(S) for _ in range(8)])),
        "n2": striped8(np.stack([np.random.permutation(U)[:V] for _ in range(8)])),
        "n3": striped8(np.stack([np.random.permutation(U) for _ in range(8)])),
    }


def reference(x_words, x_scales, d_words, d_scales, w1_words, w1_scales, mem, ga, gb, offs, k1, two, n1, n2, n3):
    d_k1 = unpack_weight(d_words, d_scales)[np.arange(K)[:, None], runs(k1, K)]
    xq = unpack_weight(x_words, x_scales)[:, unstriped(offs)]
    a = 0.0625 * (d_k1.T @ xq)
    z = f64(ga) * (a / (np.abs(a[np.arange(H)[:, None], runs(n1, H)]) + 0.5))
    x_two = unpack_weight(x_words, x_scales)[:, unstriped(two)]
    b = unpack_fp4(w1_words, w1_scales).T @ x_two
    pg = f64(mem).copy()
    pg[np.arange(H)[:, None], runs(n2, H)] = b
    z2 = f64(gb) * pg
    s = 0.0625 * ((mxq(z, 0, "e4m3").T @ mxq(z2, 0, "e4m3")))
    st = s - (s[np.arange(S)[:, None], runs(n3, S)])
    out_0 = st - (0.5 * (st[np.arange(S)[:, None], runs(n3, S)]))
    return (out_0,) + planes(out_0)

@@ -1,0 +1,239 @@
+from contextlib import ExitStack
+
+import concourse.mybir as mybir
+
+F32 = mybir.dt.float32
+BF16 = mybir.dt.bfloat16
+I32 = mybir.dt.int32
+U32 = mybir.dt.uint32
+U16 = mybir.dt.uint16
+U8 = mybir.dt.uint8
+FP8X4 = mybir.dt.float8_e4m3fn_x4
+FP4X4 = mybir.dt.float4_e2m1fn_x4
+ACT = mybir.ActivationFunctionType
+MULT = mybir.AluOpType.mult
+SUB = mybir.AluOpType.subtract
+
+P = 128
+PACK = 4
+K, T, S, V, G, H, U = 512, 1024, 512, 512, 2048, 512, 1024
+BANK = 512
+PER_COL = 16
+OUT_CHUNKS = (512, 256, 256)
+
+FLOPS = 2 * K * H * S + 2 * K * H * V + 2 * H * S * U
+
+
+def tile_picked_ckqnormpagetwice_none_po_kernel(
+    tc, x_words, x_scales, d_words, d_scales, w1_words, w1_scales, mem, ga, gb, offs, k1, two, n1, n2, n3, out_0, out_1, out_2
+):
+    nc = tc.nc
+    with ExitStack() as ctx:
+        lists = ctx.enter_context(tc.tile_pool(name="lists", bufs=1))
+        sb = ctx.enter_context(tc.tile_pool(name="sb", bufs=1))
+        ps = ctx.enter_context(tc.psum_pool(name="ps", bufs=1))
+
+        def tile(shape, dtype, name, tag=None):
+            return sb.tile(shape, dtype, name=name, tag=tag or name, align_bytes=64)
+
+        def bank(i):
+            return ps.tile([P, BANK], F32, name="bank%d" % i)
+
+        def load_list(src, name):
+            held = lists.tile(list(src.shape), U16, name=name)
+            nc.sync.dma_start(held[:], src)
+            return held
+
+        def entries(held, first, count):
+            return held[:, first // PER_COL : (first + count) // PER_COL]
+
+        xs_win = tile([P, T], U8, "xs_win")
+        ds_win = tile([P, G], U8, "ds_win")
+        ws_raw = tile([P, H], U8, "ws_raw")
+        ds = tile([P, H], U8, "ds")
+        nc.gpsimd.memset(xs_win[:].bitcast(I32), 0)
+        nc.gpsimd.memset(ws_raw[:].bitcast(I32), 0)
+        nc.vector.memset(ds_win[:].bitcast(I32), 0)
+        nc.vector.memset(ds[:].bitcast(I32), 0)
+        half = tile([P, 1], F32, "half")
+        warm = tile([P, 1], F32, "warm")
+        nc.vector.memset(half[:], 0.5)
+        nc.scalar.activation(warm[:], half[:], ACT.Ln)
+
+        two_l = load_list(two, "two_l")
+        xw_win = tile([P, T], I32, "xw_win")
+        nc.sync.dma_start(xw_win[:], x_words[0].rearrange("p n t -> p (n t)").bitcast(I32))
+        for j in range(PACK):
+            nc.sync.dma_start(xs_win[j:P:32, :].bitcast(I32), x_scales[0].rearrange("(q j) c -> j q c", j=PACK)[j].bitcast(I32))
+        ww_raw = tile([P, 2 * H], U8, "ww_raw")
+        nc.sync.dma_start(ww_raw[:].bitcast(I32), w1_words[0].bitcast(I32))
+        for j in range(PACK):
+            nc.sync.dma_start(ws_raw[j:P:32, :].bitcast(I32), w1_scales[0].rearrange("(q j) c -> j q c", j=PACK)[j].bitcast(I32))
+        k1_l = load_list(k1, "k1_l")
+        nc.sync.dma_start(ds_win[0:P:8, :].bitcast(I32), d_scales[0].bitcast(I32))
+        offs_l = load_list(offs, "offs_l")
+        dw_win = tile([P, G], I32, "dw_win")
+        nc.sync.dma_start(dw_win[:], d_words[0].rearrange("p n t -> p (n t)").bitcast(I32))
+        n2_l = load_list(n2, "n2_l")
+        ga_t = tile([P, PACK], F32, "ga_t")
+        gb_t = tile([P, PACK], F32, "gb_t")
+        nc.scalar.dma_start(gb_t[:], gb.rearrange("(p t) o -> p (t o)", t=PACK))
+        nc.scalar.dma_start(ga_t[:], ga.rearrange("(p t) o -> p (t o)", t=PACK))
+        ga_16th = tile([P, PACK], F32, "ga_16th")
+        nc.gpsimd.tensor_scalar(ga_16th[:], ga_t[:], 0.0625, 1.0, MULT, MULT)
+        mem_rows = mem.rearrange("(p t) w -> t p w", t=PACK)
+
+        def load_page(t, tag):
+            held = tile([P, U], F32, "page%d" % t, tag)
+            nc.sync.dma_start(held[:], mem_rows[t])
+            return held
+
+        page = [load_page(0, None)]
+
+        ww = tile([P, 2 * H], U8, "ww")
+        ws = tile([P, H], U8, "ws")
+        nc.vector.tensor_copy(ww[:].rearrange("p (t m e) -> p t m e", t=PACK, e=2), ww_raw[:].rearrange("p (m t e) -> p t m e", t=PACK, e=2))
+        page.append(load_page(1, "ww_raw"))
+        x2w = tile([P, V], U32, "x2w")
+        x2s = tile([P, V], U8, "x2s")
+        nc.vector.tensor_copy(x2w[:], xw_win[:].bitcast(U32).indirect(two_l[:]))
+        nc.vector.tensor_copy(x2s[:], xs_win[:].indirect(two_l[:]))
+        nc.gpsimd.tensor_copy(ws[:].rearrange("p (t m) -> p t m", t=PACK), ws_raw[:].rearrange("p (m t) -> p t m", t=PACK))
+
+        ds_picked = tile([P, H], U8, "ds_picked")
+        ds_dealt = tile([P, H], U8, "ds_dealt")
+        nc.vector.tensor_copy(ds_picked[:], ds_win[:].indirect(k1_l[:]))
+        nc.vector.tensor_copy(ds_dealt[:].rearrange("p (t m) -> p t m", t=PACK), ds_picked[:].rearrange("p (m t) -> p t m", t=PACK))
+        for j in range(PACK):
+            queue = nc.sync if j % 2 == 0 else nc.scalar
+            queue.dma_start(ds[j:P:32, :].bitcast(I32), ds_dealt[8 * j : P : 32, :].bitcast(I32))
+        n1_l = load_list(n1, "n1_l")
+        n3_l = load_list(n3, "n3_l")
+
+        b_sb = [tile([P, V], F32, "b%d" % t) for t in range(PACK)]
+        for t in range(PACK):
+            acc = bank(t)
+            nc.tensor.matmul_mx(
+                acc[:],
+                lhsT=ww[:, 2 * P * t : 2 * P * (t + 1)].bitcast(FP4X4),
+                lhsT_scale=ws[:, P * t : P * (t + 1)],
+                rhs=x2w[:].bitcast(FP8X4),
+                rhs_scale=x2s[:],
+                start=True,
+                stop=True,
+            )
+            nc.scalar.copy(b_sb[t][:], acc[:])
+
+        xqw = tile([P, S], U32, "xqw")
+        xqs = tile([P, S], U8, "xqs")
+        nc.vector.tensor_copy(xqw[:], xw_win[:].bitcast(U32).indirect(offs_l[:]))
+        nc.vector.tensor_copy(xqs[:], xs_win[:].indirect(offs_l[:]))
+        dw_picked = tile([P, H], U32, "dw_picked")
+        dw = tile([P, H], U32, "dw")
+        nc.vector.tensor_copy(dw_picked[:], dw_win[:].bitcast(U32).indirect(k1_l[:]))
+        nc.vector.tensor_copy(dw[:].rearrange("p (t m) -> p t m", t=PACK), dw_picked[:].rearrange("p (m t) -> p t m", t=PACK))
+
+        page.append(load_page(2, "xw_win"))
+        page.append(load_page(3, "dw_win"))
+        a_acc = []
+        size = tile([P, PACK, S], F32, "size")
+        ln_den = [tile([P, S], F32, "ln_den%d" % t) for t in range(PACK)]
+        inv_den = tile([P, PACK, S], F32, "inv_den")
+        for t in range(PACK):
+            acc = bank(PACK + t)
+            nc.tensor.matmul_mx(
+                acc[:],
+                lhsT=dw[:, P * t : P * (t + 1)].bitcast(FP8X4),
+                lhsT_scale=ds[:, P * t : P * (t + 1)],
+                rhs=xqw[:].bitcast(FP8X4),
+                rhs_scale=xqs[:],
+                start=True,
+                stop=True,
+            )
+            a_acc.append(acc)
+            nc.scalar.activation(size[:, t, :], acc[:], ACT.Abs, scale=0.0625)
+        for t in range(PACK):
+            nc.scalar.activation(ln_den[t][:], size[:, t, :], ACT.Ln, bias=half[:])
+        for t in range(PACK):
+            for c in range(0, S, S // 2):
+                nc.scalar.activation(
+                    inv_den[:, t, c : c + S // 2], ln_den[t][:].indirect(entries(n1_l, c, S // 2)), ACT.Exp, scale=-1.0
+                )
+
+        z2_in = tile([P, U, PACK], BF16, "z2_in")
+        for t in range(PACK):
+            nc.vector.tensor_copy(page[t][:].indirect(n2_l[:]), b_sb[t][:])
+            nc.gpsimd.tensor_scalar(z2_in[:, :, t], page[t][:], gb_t[:, t : t + 1], 1.0, MULT, MULT)
+
+        z_rows = tile([P, PACK, S], BF16, "z_rows")
+        for t in range(PACK):
+            nc.vector.scalar_tensor_tensor(z_rows[:, t, :], a_acc[t][:], ga_16th[:, t : t + 1], inv_den[:, t, :], MULT, MULT)
+        z_in = tile([P, S, PACK], BF16, "z_in")
+        nc.vector.tensor_copy(
+            z_in[:].rearrange("p (u m) t -> p m t u", u=PACK), z_rows[:].rearrange("p t (m u) -> p m t u", u=PACK)
+        )
+        zw = tile([P, S], U32, "zw")
+        zs = tile([P, S], U8, "zs")
+        nc.vector.quantize_mx(out=zw[:].bitcast(FP8X4), scales=zs[:], in_=z_in[:].rearrange("p j t -> p (j t)"))
+        z2w = tile([P, U], U32, "z2w")
+        z2s = tile([P, U], U8, "z2s")
+        for c in range(0, U, BANK):
+            nc.vector.quantize_mx(
+                out=z2w[:, c : c + BANK].bitcast(FP8X4), scales=z2s[:, c : c + BANK], in_=z2_in[:, c : c + BANK, :].rearrange("p w t -> p (w t)")
+            )
+
+        s_win = [tile([P, U], F32, "s_win%d" % t) for t in range(PACK)]
+        s_own = [tile([P, U], F32, "s_own%d" % t) for t in range(PACK)]
+        st_win = [tile([P, U], F32, "st_win%d" % t) for t in range(PACK)]
+        st_own = [tile([P, U], F32, "st_own%d" % t) for t in range(PACK)]
+        for t in range(PACK):
+            accs = []
+            for h in range(U // BANK):
+                cols = slice(h * BANK, (h + 1) * BANK)
+                acc = bank(2 * t + h)
+                nc.tensor.matmul_mx(
+                    acc[:],
+                    lhsT=zw[:, P * t : P * (t + 1)].bitcast(FP8X4),
+                    lhsT_scale=zs[:, P * t : P * (t + 1)],
+                    rhs=z2w[:, cols].bitcast(FP8X4),
+                    rhs_scale=z2s[:, cols],
+                    start=True,
+                    stop=True,
+                )
+                nc.scalar.activation(s_win[t][:, cols], acc[:], ACT.Copy, scale=0.03125)
+                accs.append(acc)
+            for h in range(U // BANK):
+                cols = slice(h * BANK, (h + 1) * BANK)
+                if t == 0 and h == 0:
+                    nc.vector.tensor_scalar(s_own[t][:, cols], accs[h][:], 0.03125, None, MULT)
+                else:
+                    nc.scalar.activation(s_own[t][:, cols], accs[h][:], ACT.Copy, scale=0.03125)
+            for h in range(U // BANK):
+                cols = slice(h * BANK, (h + 1) * BANK)
+                nc.vector.tensor_tensor(st_win[t][:, cols], s_win[t][:].indirect(entries(n3_l, h * BANK, BANK)), s_own[t][:, cols], SUB)
+        for t in range(PACK):
+            for h in range(U // BANK):
+                cols = slice(h * BANK, (h + 1) * BANK)
+                nc.scalar.activation(st_own[t][:, cols], st_win[t][:, cols], ACT.Copy, scale=2.0)
+
+        yw = tile([P, U], U32, "yw")
+        ys = tile([P, U], U8, "ys")
+        out_rows = out_0.rearrange("(p t) w -> p t w", t=PACK)
+        out_words = out_1[0].rearrange("p n t -> p (n t)").bitcast(I32)
+        first = 0
+        for i, width in enumerate(OUT_CHUNKS):
+            cols = slice(first, first + width)
+            y = tile([P, PACK, width], F32, "y%d" % i)
+            y_in = tile([P, width, PACK], BF16, "y_in%d" % i)
+            for t in range(PACK):
+                nc.vector.tensor_tensor(y[:, t, :], st_win[t][:].indirect(entries(n3_l, first, width)), st_own[t][:, cols], SUB)
+            nc.sync.dma_start(out_rows[:, :, cols], y[:])
+            if i == len(OUT_CHUNKS) - 1:
+                nc.vector.tensor_copy(y_in[:], y[:].rearrange("p t w -> p w t"))
+            else:
+                nc.scalar.copy(y_in[:], y[:].rearrange("p t w -> p w t"))
+            nc.vector.quantize_mx(out=yw[:, cols].bitcast(FP8X4), scales=ys[:, cols], in_=y_in[:].rearrange("p w t -> p (w t)"))
+            nc.sync.dma_start(out_words[:, cols], yw[:, cols].bitcast(I32))
+            first = first + width
+        for j in range(PACK):
+            nc.scalar.dma_start(out_2[0].rearrange("(q j) c -> j q c", j=PACK)[j].bitcast(I32), ys[j:P:32, :].bitcast(I32))

@@ -1,6 +1,7 @@
 from contextlib import ExitStack
 
 import concourse.mybir as mybir
+from concourse.masks import make_identity
 
 F32 = mybir.dt.float32
 BF16 = mybir.dt.bfloat16
@@ -19,7 +20,7 @@ PACK = 4
 K, T, S, V, G, H, U = 512, 1024, 512, 512, 2048, 512, 1024
 BANK = 512
 PER_COL = 16
-OUT_CHUNKS = (512, 256, 256)
+CHUNK = 256
 
 FLOPS = 2 * K * H * S + 2 * K * H * V + 2 * H * S * U
 
@@ -51,10 +52,13 @@ def tile_picked_ckqnormpagetwice_none_po_kernel(
         ds_win = tile([P, G], U8, "ds_win")
         ws_raw = tile([P, H], U8, "ws_raw")
         ds = tile([P, H], U8, "ds")
+        nc.gpsimd.memset(ds_win[:].bitcast(I32), 0)
         nc.gpsimd.memset(xs_win[:].bitcast(I32), 0)
-        nc.gpsimd.memset(ws_raw[:].bitcast(I32), 0)
-        nc.vector.memset(ds_win[:].bitcast(I32), 0)
-        nc.vector.memset(ds[:].bitcast(I32), 0)
+        nc.vector.memset(ws_raw[:].bitcast(I32), 0)
+        gain_rows = tile([P, P], F32, "gain_rows")
+        nc.vector.memset(gain_rows[:], 0.0)
+        identity = tile([P, P], F32, "identity")
+        make_identity(nc, identity[:])
         half = tile([P, 1], F32, "half")
         warm = tile([P, 1], F32, "warm")
         nc.vector.memset(half[:], 0.5)
@@ -63,54 +67,57 @@ def tile_picked_ckqnormpagetwice_none_po_kernel(
         two_l = load_list(two, "two_l")
         xw_win = tile([P, T], I32, "xw_win")
         nc.sync.dma_start(xw_win[:], x_words[0].rearrange("p n t -> p (n t)").bitcast(I32))
-        for j in range(PACK):
-            nc.sync.dma_start(xs_win[j:P:32, :].bitcast(I32), x_scales[0].rearrange("(q j) c -> j q c", j=PACK)[j].bitcast(I32))
+        offs_l = load_list(offs, "offs_l")
+        k1_l = load_list(k1, "k1_l")
         ww_raw = tile([P, 2 * H], U8, "ww_raw")
         nc.sync.dma_start(ww_raw[:].bitcast(I32), w1_words[0].bitcast(I32))
+        n2_l = load_list(n2, "n2_l")
+        n1_l = load_list(n1, "n1_l")
+        n3_l = load_list(n3, "n3_l")
+        nc.sync.dma_start(ds_win[0:P:8, :].bitcast(I32), d_scales[0].bitcast(I32))
+        for j in range(PACK):
+            nc.sync.dma_start(xs_win[j:P:32, :].bitcast(I32), x_scales[0].rearrange("(q j) c -> j q c", j=PACK)[j].bitcast(I32))
+        dw_win = tile([P, G], I32, "dw_win", "warm")
+        nc.sync.dma_start(dw_win[:], d_words[0].rearrange("p n t -> p (n t)").bitcast(I32))
         for j in range(PACK):
             nc.sync.dma_start(ws_raw[j:P:32, :].bitcast(I32), w1_scales[0].rearrange("(q j) c -> j q c", j=PACK)[j].bitcast(I32))
-        k1_l = load_list(k1, "k1_l")
-        nc.sync.dma_start(ds_win[0:P:8, :].bitcast(I32), d_scales[0].bitcast(I32))
-        offs_l = load_list(offs, "offs_l")
-        dw_win = tile([P, G], I32, "dw_win")
-        nc.sync.dma_start(dw_win[:], d_words[0].rearrange("p n t -> p (n t)").bitcast(I32))
-        n2_l = load_list(n2, "n2_l")
-        ga_t = tile([P, PACK], F32, "ga_t")
-        gb_t = tile([P, PACK], F32, "gb_t")
-        nc.scalar.dma_start(gb_t[:], gb.rearrange("(p t) o -> p (t o)", t=PACK))
-        nc.scalar.dma_start(ga_t[:], ga.rearrange("(p t) o -> p (t o)", t=PACK))
-        ga_16th = tile([P, PACK], F32, "ga_16th")
-        nc.gpsimd.tensor_scalar(ga_16th[:], ga_t[:], 0.0625, 1.0, MULT, MULT)
-        mem_rows = mem.rearrange("(p t) w -> t p w", t=PACK)
+        mem_rows = mem.rearrange("(g t r) w -> t g r w", t=PACK, r=8)
+
+        def deal(engine, dst, src):
+            engine.tensor_copy(dst.rearrange("p (t g r) -> p t g r", t=PACK, g=16), src.rearrange("p (g t r) -> p t g r", t=PACK, g=16))
 
         def load_page(t, tag):
             held = tile([P, U], F32, "page%d" % t, tag)
             nc.sync.dma_start(held[:], mem_rows[t])
             return held
 
-        page = [load_page(0, None)]
-
-        ww = tile([P, 2 * H], U8, "ww")
-        ws = tile([P, H], U8, "ws")
-        nc.vector.tensor_copy(ww[:].rearrange("p (t m e) -> p t m e", t=PACK, e=2), ww_raw[:].rearrange("p (m t e) -> p t m e", t=PACK, e=2))
-        page.append(load_page(1, "ww_raw"))
-        x2w = tile([P, V], U32, "x2w")
-        x2s = tile([P, V], U8, "x2s")
-        nc.vector.tensor_copy(x2w[:], xw_win[:].bitcast(U32).indirect(two_l[:]))
-        nc.vector.tensor_copy(x2s[:], xs_win[:].indirect(two_l[:]))
-        nc.gpsimd.tensor_copy(ws[:].rearrange("p (t m) -> p t m", t=PACK), ws_raw[:].rearrange("p (m t) -> p t m", t=PACK))
 
         ds_picked = tile([P, H], U8, "ds_picked")
         ds_dealt = tile([P, H], U8, "ds_dealt")
         nc.vector.tensor_copy(ds_picked[:], ds_win[:].indirect(k1_l[:]))
-        nc.vector.tensor_copy(ds_dealt[:].rearrange("p (t m) -> p t m", t=PACK), ds_picked[:].rearrange("p (m t) -> p t m", t=PACK))
-        for j in range(PACK):
-            queue = nc.sync if j % 2 == 0 else nc.scalar
-            queue.dma_start(ds[j:P:32, :].bitcast(I32), ds_dealt[8 * j : P : 32, :].bitcast(I32))
-        n1_l = load_list(n1, "n1_l")
-        n3_l = load_list(n3, "n3_l")
+        deal(nc.vector, ds_dealt[:].bitcast(I32), ds_picked[:].bitcast(I32))
+        deal(nc.vector, ds[:].bitcast(I32), ds_picked[:].bitcast(I32))
+        for j in range(1, PACK):
+            nc.scalar.dma_start(ds[j:P:32, :].bitcast(I32), ds_dealt[8 * j : P : 32, :].bitcast(I32))
+        page = [load_page(0, "ds_win")]
+        for i, gain in enumerate((ga, gb)):
+            nc.sync.dma_start(
+                gain_rows[PACK * i : PACK * (i + 1), :].rearrange("t (g r) -> t g r", r=8), gain.rearrange("(g t r) o -> t g (r o)", t=PACK, r=8)
+            )
+        ww = tile([P, 2 * H], U8, "ww")
+        ws = tile([P, H], U8, "ws")
+        x2w = tile([P, V], U32, "x2w")
+        x2s = tile([P, V], U8, "x2s")
+        xqw = tile([P, S], U32, "xqw")
+        xqs = tile([P, S], U8, "xqs")
+        nc.vector.tensor_copy(x2s[:], xs_win[:].indirect(two_l[:]))
+        nc.vector.tensor_copy(x2w[:], xw_win[:].bitcast(U32).indirect(two_l[:]))
+        deal(nc.gpsimd, ww[:].bitcast(I32), ww_raw[:].bitcast(I32))
+        deal(nc.gpsimd, ws[:].bitcast(I32), ws_raw[:].bitcast(I32))
+        nc.vector.tensor_copy(xqs[:], xs_win[:].indirect(offs_l[:]))
 
-        b_sb = [tile([P, V], F32, "b%d" % t) for t in range(PACK)]
+        b_acc = []
+        b_sb = [None] + [tile([P, V], F32, "b%d" % t) for t in range(1, PACK)]
         for t in range(PACK):
             acc = bank(t)
             nc.tensor.matmul_mx(
@@ -122,23 +129,28 @@ def tile_picked_ckqnormpagetwice_none_po_kernel(
                 start=True,
                 stop=True,
             )
-            nc.scalar.copy(b_sb[t][:], acc[:])
+            b_acc.append(acc)
+            if t > 0:
+                nc.scalar.copy(b_sb[t][:], acc[:])
 
-        xqw = tile([P, S], U32, "xqw")
-        xqs = tile([P, S], U8, "xqs")
+        turned = bank(1)
+        nc.tensor.transpose(turned[:, 0:P], gain_rows[:], identity[:])
+        ga_16th = tile([P, PACK], F32, "ga_16th")
+        gb_t = tile([P, PACK], F32, "gb_t")
+        nc.scalar.activation(ga_16th[:], turned[:, 0:PACK], ACT.Copy, scale=0.0625)
+        nc.scalar.copy(gb_t[:], turned[:, PACK : 2 * PACK])
         nc.vector.tensor_copy(xqw[:], xw_win[:].bitcast(U32).indirect(offs_l[:]))
-        nc.vector.tensor_copy(xqs[:], xs_win[:].indirect(offs_l[:]))
         dw_picked = tile([P, H], U32, "dw_picked")
         dw = tile([P, H], U32, "dw")
         nc.vector.tensor_copy(dw_picked[:], dw_win[:].bitcast(U32).indirect(k1_l[:]))
-        nc.vector.tensor_copy(dw[:].rearrange("p (t m) -> p t m", t=PACK), dw_picked[:].rearrange("p (m t) -> p t m", t=PACK))
+        deal(nc.vector, dw[:], dw_picked[:])
+        b_sb[0] = tile([P, V], F32, "b0", "warm")
+        nc.scalar.copy(b_sb[0][:], b_acc[0][:])
 
-        page.append(load_page(2, "xw_win"))
-        page.append(load_page(3, "dw_win"))
+
         a_acc = []
         size = tile([P, PACK, S], F32, "size")
         ln_den = [tile([P, S], F32, "ln_den%d" % t) for t in range(PACK)]
-        inv_den = tile([P, PACK, S], F32, "inv_den")
         for t in range(PACK):
             acc = bank(PACK + t)
             nc.tensor.matmul_mx(
@@ -152,18 +164,26 @@ def tile_picked_ckqnormpagetwice_none_po_kernel(
             )
             a_acc.append(acc)
             nc.scalar.activation(size[:, t, :], acc[:], ACT.Abs, scale=0.0625)
+        page.extend(load_page(t, spent) for t, spent in ((1, "dw_picked"), (2, "dw"), (3, "xqw")))
         for t in range(PACK):
             nc.scalar.activation(ln_den[t][:], size[:, t, :], ACT.Ln, bias=half[:])
+        inv_den = tile([P, PACK, S], F32, "inv_den", "size")
         for t in range(PACK):
             for c in range(0, S, S // 2):
                 nc.scalar.activation(
                     inv_den[:, t, c : c + S // 2], ln_den[t][:].indirect(entries(n1_l, c, S // 2)), ACT.Exp, scale=-1.0
                 )
 
-        z2_in = tile([P, U, PACK], BF16, "z2_in")
+        z2_pairs = [tile([P, 2, BANK, 2], BF16, "z2_pairs%d" % h, "ln_den%d" % (2 + h)) for h in range(U // BANK)]
         for t in range(PACK):
             nc.vector.tensor_copy(page[t][:].indirect(n2_l[:]), b_sb[t][:])
-            nc.gpsimd.tensor_scalar(z2_in[:, :, t], page[t][:], gb_t[:, t : t + 1], 1.0, MULT, MULT)
+            for h in range(U // BANK):
+                woven = z2_pairs[h][:, t // 2, :, t % 2]
+                slots = page[t][:, h * BANK : (h + 1) * BANK]
+                if h == 0 and t >= 2:
+                    nc.vector.tensor_scalar(woven, slots, gb_t[:, t : t + 1], None, MULT)
+                else:
+                    nc.scalar.activation(woven, slots, ACT.Copy, scale=gb_t[:, t : t + 1])
 
         z_rows = tile([P, PACK, S], BF16, "z_rows")
         for t in range(PACK):
@@ -177,10 +197,13 @@ def tile_picked_ckqnormpagetwice_none_po_kernel(
         nc.vector.quantize_mx(out=zw[:].bitcast(FP8X4), scales=zs[:], in_=z_in[:].rearrange("p j t -> p (j t)"))
         z2w = tile([P, U], U32, "z2w")
         z2s = tile([P, U], U8, "z2s")
-        for c in range(0, U, BANK):
-            nc.vector.quantize_mx(
-                out=z2w[:, c : c + BANK].bitcast(FP8X4), scales=z2s[:, c : c + BANK], in_=z2_in[:, c : c + BANK, :].rearrange("p w t -> p (w t)")
+        z2_in = tile([P, U // BANK, BANK * PACK], BF16, "z2_in")
+        for h in range(U // BANK):
+            nc.vector.tensor_copy(
+                z2_in[:, h, :].bitcast(I32).rearrange("p (c i e) -> p c e i", i=4, e=2),
+                z2_pairs[h][:].rearrange("p e w d -> p e (w d)").bitcast(I32).rearrange("p e (c i) -> p c e i", i=4),
             )
+        nc.vector.quantize_mx(out=z2w[:].bitcast(FP8X4), scales=z2s[:], in_=z2_in[:].rearrange("p h c -> p (h c)"))
 
         s_win = [tile([P, U], F32, "s_win%d" % t) for t in range(PACK)]
         s_own = [tile([P, U], F32, "s_own%d" % t) for t in range(PACK)]
@@ -211,29 +234,30 @@ def tile_picked_ckqnormpagetwice_none_po_kernel(
             for h in range(U // BANK):
                 cols = slice(h * BANK, (h + 1) * BANK)
                 nc.vector.tensor_tensor(st_win[t][:, cols], s_win[t][:].indirect(entries(n3_l, h * BANK, BANK)), s_own[t][:, cols], SUB)
-        for t in range(PACK):
-            for h in range(U // BANK):
-                cols = slice(h * BANK, (h + 1) * BANK)
+        for first in range(0, U, CHUNK):
+            for t in range(PACK):
+                cols = slice(first, first + CHUNK)
                 nc.scalar.activation(st_own[t][:, cols], st_win[t][:, cols], ACT.Copy, scale=2.0)
 
         yw = tile([P, U], U32, "yw")
         ys = tile([P, U], U8, "ys")
         out_rows = out_0.rearrange("(p t) w -> p t w", t=PACK)
         out_words = out_1[0].rearrange("p n t -> p (n t)").bitcast(I32)
-        first = 0
-        for i, width in enumerate(OUT_CHUNKS):
-            cols = slice(first, first + width)
-            y = tile([P, PACK, width], F32, "y%d" % i)
-            y_in = tile([P, width, PACK], BF16, "y_in%d" % i)
+        for i in range(U // CHUNK):
+            first = i * CHUNK
+            cols = slice(first, first + CHUNK)
+            y = tile([P, PACK, CHUNK], F32, "y%d" % i, "y_in%d" % (i - 2) if i >= 2 else None)
+            y_in = tile([P, CHUNK, PACK], BF16, "y_in%d" % i)
             for t in range(PACK):
-                nc.vector.tensor_tensor(y[:, t, :], st_win[t][:].indirect(entries(n3_l, first, width)), st_own[t][:, cols], SUB)
+                nc.vector.tensor_tensor(y[:, t, :], st_win[t][:].indirect(entries(n3_l, first, CHUNK)), st_own[t][:, cols], SUB)
             nc.sync.dma_start(out_rows[:, :, cols], y[:])
-            if i == len(OUT_CHUNKS) - 1:
-                nc.vector.tensor_copy(y_in[:], y[:].rearrange("p t w -> p w t"))
+            woven = y_in[:].rearrange("p (c i) t -> p c t i", i=4)
+            rows = y[:].rearrange("p t (c i) -> p c t i", i=4)
+            if i == U // CHUNK - 1:
+                nc.vector.tensor_copy(woven, rows)
             else:
-                nc.scalar.copy(y_in[:], y[:].rearrange("p t w -> p w t"))
+                nc.scalar.copy(woven, rows)
             nc.vector.quantize_mx(out=yw[:, cols].bitcast(FP8X4), scales=ys[:, cols], in_=y_in[:].rearrange("p w t -> p (w t)"))
             nc.sync.dma_start(out_words[:, cols], yw[:, cols].bitcast(I32))
-            first = first + width
         for j in range(PACK):
             nc.scalar.dma_start(out_2[0].rearrange("(q j) c -> j q c", j=PACK)[j].bitcast(I32), ys[j:P:32, :].bitcast(I32))

@@ -52,35 +52,35 @@ def tile_picked_ckqnormpagetwice_none_po_kernel(
         ds_win = tile([P, G], U8, "ds_win")
         ws_raw = tile([P, H], U8, "ws_raw")
         ds = tile([P, H], U8, "ds")
-        nc.gpsimd.memset(ds_win[:].bitcast(I32), 0)
-        nc.gpsimd.memset(xs_win[:].bitcast(I32), 0)
+        nc.vector.memset(xs_win[:].bitcast(I32), 0)
+        nc.vector.memset(ds_win[:].bitcast(I32), 0)
         nc.vector.memset(ws_raw[:].bitcast(I32), 0)
-        gain_rows = tile([P, P], F32, "gain_rows")
-        nc.vector.memset(gain_rows[:], 0.0)
+        nc.gpsimd.memset(ds[:].bitcast(I32), 0)
+        ww_raw = tile([P, 2 * H], U8, "ww_raw")
+        nc.gpsimd.dma_start(ww_raw[:].bitcast(I32), w1_words[0].bitcast(I32))
         identity = tile([P, P], F32, "identity")
         make_identity(nc, identity[:])
+
+        k1_l = load_list(k1, "k1_l")
+        two_l = load_list(two, "two_l")
+        xw_win = tile([P, T], I32, "xw_win")
+        nc.sync.dma_start(xw_win[:], x_words[0].rearrange("p n t -> p (n t)").bitcast(I32))
+        nc.sync.dma_start(ds_win[0:P:8, :].bitcast(I32), d_scales[0].bitcast(I32))
+        for q in range(4):
+            nc.scalar.dma_start(xs_win[32 * q : 32 * q + 4, :].bitcast(I32), x_scales[0][4 * q : 4 * q + 4, :].bitcast(I32))
+        for q in range(4):
+            nc.scalar.dma_start(ws_raw[32 * q : 32 * q + 4, :].bitcast(I32), w1_scales[0][4 * q : 4 * q + 4, :].bitcast(I32))
+        offs_l = load_list(offs, "offs_l")
+        dw_win = tile([P, G], I32, "dw_win")
+        nc.sync.dma_start(dw_win[:], d_words[0].rearrange("p n t -> p (n t)").bitcast(I32))
+        n2_l = load_list(n2, "n2_l")
+
+        gain_rows = tile([P, P], F32, "gain_rows")
+        nc.vector.memset(gain_rows[:], 0.0)
         half = tile([P, 1], F32, "half")
         warm = tile([P, 1], F32, "warm")
         nc.vector.memset(half[:], 0.5)
         nc.scalar.activation(warm[:], half[:], ACT.Ln)
-
-        two_l = load_list(two, "two_l")
-        xw_win = tile([P, T], I32, "xw_win")
-        nc.sync.dma_start(xw_win[:], x_words[0].rearrange("p n t -> p (n t)").bitcast(I32))
-        offs_l = load_list(offs, "offs_l")
-        k1_l = load_list(k1, "k1_l")
-        ww_raw = tile([P, 2 * H], U8, "ww_raw")
-        nc.sync.dma_start(ww_raw[:].bitcast(I32), w1_words[0].bitcast(I32))
-        n2_l = load_list(n2, "n2_l")
-        n1_l = load_list(n1, "n1_l")
-        n3_l = load_list(n3, "n3_l")
-        nc.sync.dma_start(ds_win[0:P:8, :].bitcast(I32), d_scales[0].bitcast(I32))
-        for j in range(PACK):
-            nc.sync.dma_start(xs_win[j:P:32, :].bitcast(I32), x_scales[0].rearrange("(q j) c -> j q c", j=PACK)[j].bitcast(I32))
-        dw_win = tile([P, G], I32, "dw_win", "warm")
-        nc.sync.dma_start(dw_win[:], d_words[0].rearrange("p n t -> p (n t)").bitcast(I32))
-        for j in range(PACK):
-            nc.sync.dma_start(ws_raw[j:P:32, :].bitcast(I32), w1_scales[0].rearrange("(q j) c -> j q c", j=PACK)[j].bitcast(I32))
         mem_rows = mem.rearrange("(g t r) w -> t g r w", t=PACK, r=8)
 
         def deal(engine, dst, src):
@@ -96,14 +96,15 @@ def tile_picked_ckqnormpagetwice_none_po_kernel(
         ds_dealt = tile([P, H], U8, "ds_dealt")
         nc.vector.tensor_copy(ds_picked[:], ds_win[:].indirect(k1_l[:]))
         deal(nc.vector, ds_dealt[:].bitcast(I32), ds_picked[:].bitcast(I32))
-        deal(nc.vector, ds[:].bitcast(I32), ds_picked[:].bitcast(I32))
-        for j in range(1, PACK):
-            nc.scalar.dma_start(ds[j:P:32, :].bitcast(I32), ds_dealt[8 * j : P : 32, :].bitcast(I32))
+        for q in range(4):
+            nc.sync.dma_start(ds[32 * q : 32 * q + 4, :].bitcast(I32), ds_dealt[32 * q : 32 * q + 32 : 8, :].bitcast(I32))
         page = [load_page(0, "ds_win")]
         for i, gain in enumerate((ga, gb)):
             nc.sync.dma_start(
                 gain_rows[PACK * i : PACK * (i + 1), :].rearrange("t (g r) -> t g r", r=8), gain.rearrange("(g t r) o -> t g (r o)", t=PACK, r=8)
             )
+        n1_l = load_list(n1, "n1_l")
+        n3_l = load_list(n3, "n3_l")
         ww = tile([P, 2 * H], U8, "ww")
         ws = tile([P, H], U8, "ws")
         x2w = tile([P, V], U32, "x2w")
@@ -136,15 +137,15 @@ def tile_picked_ckqnormpagetwice_none_po_kernel(
         turned = bank(1)
         nc.tensor.transpose(turned[:, 0:P], gain_rows[:], identity[:])
         ga_16th = tile([P, PACK], F32, "ga_16th")
-        gb_t = tile([P, PACK], F32, "gb_t")
+        gb_low = tile([P, 2], F32, "gb_low")
         nc.scalar.activation(ga_16th[:], turned[:, 0:PACK], ACT.Copy, scale=0.0625)
-        nc.scalar.copy(gb_t[:], turned[:, PACK : 2 * PACK])
+        nc.scalar.copy(gb_low[:], turned[:, PACK : PACK + 2])
         nc.vector.tensor_copy(xqw[:], xw_win[:].bitcast(U32).indirect(offs_l[:]))
         dw_picked = tile([P, H], U32, "dw_picked")
         dw = tile([P, H], U32, "dw")
         nc.vector.tensor_copy(dw_picked[:], dw_win[:].bitcast(U32).indirect(k1_l[:]))
         deal(nc.vector, dw[:], dw_picked[:])
-        b_sb[0] = tile([P, V], F32, "b0", "warm")
+        b_sb[0] = tile([P, V], F32, "b0", "dw_win")
         nc.scalar.copy(b_sb[0][:], b_acc[0][:])
 
 
@@ -174,16 +175,18 @@ def tile_picked_ckqnormpagetwice_none_po_kernel(
                     inv_den[:, t, c : c + S // 2], ln_den[t][:].indirect(entries(n1_l, c, S // 2)), ACT.Exp, scale=-1.0
                 )
 
-        z2_pairs = [tile([P, 2, BANK, 2], BF16, "z2_pairs%d" % h, "ln_den%d" % (2 + h)) for h in range(U // BANK)]
+        gb_high = tile([P, 2], F32, "gb_high", "ln_den2")
+        nc.scalar.copy(gb_high[:], turned[:, PACK + 2 : PACK + 4])
+        z2_pairs = [tile([P, 2, BANK, 2], BF16, "z2_pairs%d" % h) for h in range(U // BANK)]
         for t in range(PACK):
             nc.vector.tensor_copy(page[t][:].indirect(n2_l[:]), b_sb[t][:])
             for h in range(U // BANK):
                 woven = z2_pairs[h][:, t // 2, :, t % 2]
                 slots = page[t][:, h * BANK : (h + 1) * BANK]
-                if h == 0 and t >= 2:
-                    nc.vector.tensor_scalar(woven, slots, gb_t[:, t : t + 1], None, MULT)
+                if t < 2:
+                    nc.gpsimd.tensor_scalar(woven, slots, gb_low[:, t : t + 1], 1.0, MULT, MULT)
                 else:
-                    nc.scalar.activation(woven, slots, ACT.Copy, scale=gb_t[:, t : t + 1])
+                    nc.scalar.activation(woven, slots, ACT.Copy, scale=gb_high[:, t - 2 : t - 1])
 
         z_rows = tile([P, PACK, S], BF16, "z_rows")
         for t in range(PACK):
@@ -197,13 +200,15 @@ def tile_picked_ckqnormpagetwice_none_po_kernel(
         nc.vector.quantize_mx(out=zw[:].bitcast(FP8X4), scales=zs[:], in_=z_in[:].rearrange("p j t -> p (j t)"))
         z2w = tile([P, U], U32, "z2w")
         z2s = tile([P, U], U8, "z2s")
-        z2_in = tile([P, U // BANK, BANK * PACK], BF16, "z2_in")
+        z2_in = [tile([P, BANK * PACK], BF16, "z2_in%d" % h) for h in range(U // BANK)]
         for h in range(U // BANK):
             nc.vector.tensor_copy(
-                z2_in[:, h, :].bitcast(I32).rearrange("p (c i e) -> p c e i", i=4, e=2),
+                z2_in[h][:].bitcast(I32).rearrange("p (c i e) -> p c e i", i=4, e=2),
                 z2_pairs[h][:].rearrange("p e w d -> p e (w d)").bitcast(I32).rearrange("p e (c i) -> p c e i", i=4),
             )
-        nc.vector.quantize_mx(out=z2w[:].bitcast(FP8X4), scales=z2s[:], in_=z2_in[:].rearrange("p h c -> p (h c)"))
+        for h in range(U // BANK):
+            cols = slice(h * BANK, (h + 1) * BANK)
+            nc.vector.quantize_mx(out=z2w[:, cols].bitcast(FP8X4), scales=z2s[:, cols], in_=z2_in[h][:])
 
         s_win = [tile([P, U], F32, "s_win%d" % t) for t in range(PACK)]
         s_own = [tile([P, U], F32, "s_own%d" % t) for t in range(PACK)]
@@ -259,5 +264,5 @@ def tile_picked_ckqnormpagetwice_none_po_kernel(
                 nc.scalar.copy(woven, rows)
             nc.vector.quantize_mx(out=yw[:, cols].bitcast(FP8X4), scales=ys[:, cols], in_=y_in[:].rearrange("p w t -> p (w t)"))
             nc.sync.dma_start(out_words[:, cols], yw[:, cols].bitcast(I32))
-        for j in range(PACK):
-            nc.scalar.dma_start(out_2[0].rearrange("(q j) c -> j q c", j=PACK)[j].bitcast(I32), ys[j:P:32, :].bitcast(I32))
+        for q in range(4):
+            nc.scalar.dma_start(out_2[0][4 * q : 4 * q + 4, :].bitcast(I32), ys[32 * q : 32 * q + 4, :].bitcast(I32))

@@ -97,7 +97,7 @@ def tile_picked_ckqnormpagetwice_none_po_kernel(
         nc.vector.tensor_copy(ds_picked[:], ds_win[:].indirect(k1_l[:]))
         deal(nc.vector, ds_dealt[:].bitcast(I32), ds_picked[:].bitcast(I32))
         for q in range(4):
-            nc.sync.dma_start(ds[32 * q : 32 * q + 4, :].bitcast(I32), ds_dealt[32 * q : 32 * q + 32 : 8, :].bitcast(I32))
+            nc.scalar.dma_start(ds[32 * q : 32 * q + 4, :].bitcast(I32), ds_dealt[32 * q : 32 * q + 32 : 8, :].bitcast(I32))
         page = [load_page(0, "ds_win")]
         for i, gain in enumerate((ga, gb)):
             nc.sync.dma_start(
@@ -117,8 +117,7 @@ def tile_picked_ckqnormpagetwice_none_po_kernel(
         deal(nc.gpsimd, ws[:].bitcast(I32), ws_raw[:].bitcast(I32))
         nc.vector.tensor_copy(xqs[:], xs_win[:].indirect(offs_l[:]))
 
-        b_acc = []
-        b_sb = [None] + [tile([P, V], F32, "b%d" % t) for t in range(1, PACK)]
+        b_sb = [tile([P, V], F32, "b%d" % t) for t in range(PACK)]
         for t in range(PACK):
             acc = bank(t)
             nc.tensor.matmul_mx(
@@ -130,9 +129,7 @@ def tile_picked_ckqnormpagetwice_none_po_kernel(
                 start=True,
                 stop=True,
             )
-            b_acc.append(acc)
-            if t > 0:
-                nc.scalar.copy(b_sb[t][:], acc[:])
+            nc.scalar.copy(b_sb[t][:], acc[:])
 
         turned = bank(1)
         nc.tensor.transpose(turned[:, 0:P], gain_rows[:], identity[:])
@@ -145,8 +142,6 @@ def tile_picked_ckqnormpagetwice_none_po_kernel(
         dw = tile([P, H], U32, "dw")
         nc.vector.tensor_copy(dw_picked[:], dw_win[:].bitcast(U32).indirect(k1_l[:]))
         deal(nc.vector, dw[:], dw_picked[:])
-        b_sb[0] = tile([P, V], F32, "b0", "dw_win")
-        nc.scalar.copy(b_sb[0][:], b_acc[0][:])
 
 
         a_acc = []
@@ -165,7 +160,7 @@ def tile_picked_ckqnormpagetwice_none_po_kernel(
             )
             a_acc.append(acc)
             nc.scalar.activation(size[:, t, :], acc[:], ACT.Abs, scale=0.0625)
-        page.extend(load_page(t, spent) for t, spent in ((1, "dw_picked"), (2, "dw"), (3, "xqw")))
+        page.extend(load_page(t, spent) for t, spent in ((1, "xs_win"), (2, "xw_win"), (3, "dw_win")))
         for t in range(PACK):
             nc.scalar.activation(ln_den[t][:], size[:, t, :], ACT.Ln, bias=half[:])
         inv_den = tile([P, PACK, S], F32, "inv_den", "size")
@@ -192,7 +187,7 @@ def tile_picked_ckqnormpagetwice_none_po_kernel(
         for t in range(PACK):
             nc.vector.scalar_tensor_tensor(z_rows[:, t, :], a_acc[t][:], ga_16th[:, t : t + 1], inv_den[:, t, :], MULT, MULT)
         z_in = tile([P, S, PACK], BF16, "z_in")
-        nc.vector.tensor_copy(
+        nc.scalar.copy(
             z_in[:].rearrange("p (u m) t -> p m t u", u=PACK), z_rows[:].rearrange("p t (m u) -> p m t u", u=PACK)
         )
         zw = tile([P, S], U32, "zw")
@@ -232,7 +227,7 @@ def tile_picked_ckqnormpagetwice_none_po_kernel(
                 accs.append(acc)
             for h in range(U // BANK):
                 cols = slice(h * BANK, (h + 1) * BANK)
-                if t == 0 and h == 0:
+                if t == 0:
                     nc.vector.tensor_scalar(s_own[t][:, cols], accs[h][:], 0.03125, None, MULT)
                 else:
                     nc.scalar.activation(s_own[t][:, cols], accs[h][:], ACT.Copy, scale=0.03125)

from contextlib import ExitStack

import concourse.mybir as mybir
from concourse.masks import make_identity

F32 = mybir.dt.float32
BF16 = mybir.dt.bfloat16
I32 = mybir.dt.int32
U32 = mybir.dt.uint32
U16 = mybir.dt.uint16
U8 = mybir.dt.uint8
FP8X4 = mybir.dt.float8_e4m3fn_x4
FP4X4 = mybir.dt.float4_e2m1fn_x4
ACT = mybir.ActivationFunctionType
MULT = mybir.AluOpType.mult
SUB = mybir.AluOpType.subtract

P = 128
PACK = 4
K, T, S, V, G, H, U = 512, 1024, 512, 512, 2048, 512, 1024
BANK = 512
PER_COL = 16
CHUNK = 256

FLOPS = 2 * K * H * S + 2 * K * H * V + 2 * H * S * U


def tile_picked_ckqnormpagetwice_none_po_kernel(
    tc, x_words, x_scales, d_words, d_scales, w1_words, w1_scales, mem, ga, gb, offs, k1, two, n1, n2, n3, out_0, out_1, out_2
):
    nc = tc.nc
    with ExitStack() as ctx:
        lists = ctx.enter_context(tc.tile_pool(name="lists", bufs=1))
        sb = ctx.enter_context(tc.tile_pool(name="sb", bufs=1))
        ps = ctx.enter_context(tc.psum_pool(name="ps", bufs=1))

        def tile(shape, dtype, name, tag=None):
            return sb.tile(shape, dtype, name=name, tag=tag or name, align_bytes=64)

        def bank(i):
            return ps.tile([P, BANK], F32, name="bank%d" % i)

        def load_list(src, name):
            held = lists.tile(list(src.shape), U16, name=name)
            nc.sync.dma_start(held[:], src)
            return held

        def entries(held, first, count):
            return held[:, first // PER_COL : (first + count) // PER_COL]

        xs_win = tile([P, T], U8, "xs_win")
        ds_win = tile([P, G], U8, "ds_win")
        ws_raw = tile([P, H], U8, "ws_raw")
        ds = tile([P, H], U8, "ds")
        nc.vector.memset(xs_win[:].bitcast(I32), 0)
        nc.vector.memset(ds_win[:].bitcast(I32), 0)
        nc.vector.memset(ws_raw[:].bitcast(I32), 0)
        nc.gpsimd.memset(ds[:].bitcast(I32), 0)
        ww_raw = tile([P, 2 * H], U8, "ww_raw")
        nc.gpsimd.dma_start(ww_raw[:].bitcast(I32), w1_words[0].bitcast(I32))
        identity = tile([P, P], F32, "identity")
        make_identity(nc, identity[:])

        k1_l = load_list(k1, "k1_l")
        two_l = load_list(two, "two_l")
        xw_win = tile([P, T], I32, "xw_win")
        nc.sync.dma_start(xw_win[:], x_words[0].rearrange("p n t -> p (n t)").bitcast(I32))
        nc.sync.dma_start(ds_win[0:P:8, :].bitcast(I32), d_scales[0].bitcast(I32))
        for q in range(4):
            nc.scalar.dma_start(xs_win[32 * q : 32 * q + 4, :].bitcast(I32), x_scales[0][4 * q : 4 * q + 4, :].bitcast(I32))
        for q in range(4):
            nc.scalar.dma_start(ws_raw[32 * q : 32 * q + 4, :].bitcast(I32), w1_scales[0][4 * q : 4 * q + 4, :].bitcast(I32))
        offs_l = load_list(offs, "offs_l")
        dw_win = tile([P, G], I32, "dw_win")
        nc.sync.dma_start(dw_win[:], d_words[0].rearrange("p n t -> p (n t)").bitcast(I32))
        n2_l = load_list(n2, "n2_l")

        gain_rows = tile([P, P], F32, "gain_rows")
        nc.vector.memset(gain_rows[:], 0.0)
        half = tile([P, 1], F32, "half")
        warm = tile([P, 1], F32, "warm")
        nc.vector.memset(half[:], 0.5)
        nc.scalar.activation(warm[:], half[:], ACT.Ln)
        mem_rows = mem.rearrange("(g t r) w -> t g r w", t=PACK, r=8)

        def deal(engine, dst, src):
            engine.tensor_copy(dst.rearrange("p (t g r) -> p t g r", t=PACK, g=16), src.rearrange("p (g t r) -> p t g r", t=PACK, g=16))

        def load_page(t, tag):
            held = tile([P, U], F32, "page%d" % t, tag)
            nc.sync.dma_start(held[:], mem_rows[t])
            return held


        ds_picked = tile([P, H], U8, "ds_picked")
        ds_dealt = tile([P, H], U8, "ds_dealt")
        nc.vector.tensor_copy(ds_picked[:], ds_win[:].indirect(k1_l[:]))
        deal(nc.vector, ds_dealt[:].bitcast(I32), ds_picked[:].bitcast(I32))
        for q in range(4):
            nc.scalar.dma_start(ds[32 * q : 32 * q + 4, :].bitcast(I32), ds_dealt[32 * q : 32 * q + 32 : 8, :].bitcast(I32))
        page = [load_page(0, "ds_win")]
        for i, gain in enumerate((ga, gb)):
            nc.sync.dma_start(
                gain_rows[PACK * i : PACK * (i + 1), :].rearrange("t (g r) -> t g r", r=8), gain.rearrange("(g t r) o -> t g (r o)", t=PACK, r=8)
            )
        n1_l = load_list(n1, "n1_l")
        n3_l = load_list(n3, "n3_l")
        ww = tile([P, 2 * H], U8, "ww")
        ws = tile([P, H], U8, "ws")
        x2w = tile([P, V], U32, "x2w")
        x2s = tile([P, V], U8, "x2s")
        xqw = tile([P, S], U32, "xqw")
        xqs = tile([P, S], U8, "xqs")
        nc.vector.tensor_copy(x2s[:], xs_win[:].indirect(two_l[:]))
        nc.vector.tensor_copy(x2w[:], xw_win[:].bitcast(U32).indirect(two_l[:]))
        deal(nc.gpsimd, ww[:].bitcast(I32), ww_raw[:].bitcast(I32))
        deal(nc.gpsimd, ws[:].bitcast(I32), ws_raw[:].bitcast(I32))
        nc.vector.tensor_copy(xqs[:], xs_win[:].indirect(offs_l[:]))

        b_sb = [tile([P, V], F32, "b%d" % t) for t in range(PACK)]
        for t in range(PACK):
            acc = bank(t)
            nc.tensor.matmul_mx(
                acc[:],
                lhsT=ww[:, 2 * P * t : 2 * P * (t + 1)].bitcast(FP4X4),
                lhsT_scale=ws[:, P * t : P * (t + 1)],
                rhs=x2w[:].bitcast(FP8X4),
                rhs_scale=x2s[:],
                start=True,
                stop=True,
            )
            nc.scalar.copy(b_sb[t][:], acc[:])

        turned = bank(1)
        nc.tensor.transpose(turned[:, 0:P], gain_rows[:], identity[:])
        ga_16th = tile([P, PACK], F32, "ga_16th")
        gb_low = tile([P, 2], F32, "gb_low")
        nc.scalar.activation(ga_16th[:], turned[:, 0:PACK], ACT.Copy, scale=0.0625)
        nc.scalar.copy(gb_low[:], turned[:, PACK : PACK + 2])
        nc.vector.tensor_copy(xqw[:], xw_win[:].bitcast(U32).indirect(offs_l[:]))
        dw_picked = tile([P, H], U32, "dw_picked")
        dw = tile([P, H], U32, "dw")
        nc.vector.tensor_copy(dw_picked[:], dw_win[:].bitcast(U32).indirect(k1_l[:]))
        deal(nc.vector, dw[:], dw_picked[:])


        a_acc = []
        size = tile([P, PACK, S], F32, "size")
        ln_den = [tile([P, S], F32, "ln_den%d" % t) for t in range(PACK)]
        for t in range(PACK):
            acc = bank(PACK + t)
            nc.tensor.matmul_mx(
                acc[:],
                lhsT=dw[:, P * t : P * (t + 1)].bitcast(FP8X4),
                lhsT_scale=ds[:, P * t : P * (t + 1)],
                rhs=xqw[:].bitcast(FP8X4),
                rhs_scale=xqs[:],
                start=True,
                stop=True,
            )
            a_acc.append(acc)
            nc.scalar.activation(size[:, t, :], acc[:], ACT.Abs, scale=0.0625)
        page.extend(load_page(t, spent) for t, spent in ((1, "xs_win"), (2, "xw_win"), (3, "dw_win")))
        for t in range(PACK):
            nc.scalar.activation(ln_den[t][:], size[:, t, :], ACT.Ln, bias=half[:])
        inv_den = tile([P, PACK, S], F32, "inv_den", "size")
        for t in range(PACK):
            for c in range(0, S, S // 2):
                nc.scalar.activation(
                    inv_den[:, t, c : c + S // 2], ln_den[t][:].indirect(entries(n1_l, c, S // 2)), ACT.Exp, scale=-1.0
                )

        gb_high = tile([P, 2], F32, "gb_high", "ln_den2")
        nc.scalar.copy(gb_high[:], turned[:, PACK + 2 : PACK + 4])
        z2_pairs = [tile([P, 2, BANK, 2], BF16, "z2_pairs%d" % h) for h in range(U // BANK)]
        for t in range(PACK):
            nc.vector.tensor_copy(page[t][:].indirect(n2_l[:]), b_sb[t][:])
            for h in range(U // BANK):
                woven = z2_pairs[h][:, t // 2, :, t % 2]
                slots = page[t][:, h * BANK : (h + 1) * BANK]
                if t < 2:
                    nc.gpsimd.tensor_scalar(woven, slots, gb_low[:, t : t + 1], 1.0, MULT, MULT)
                else:
                    nc.scalar.activation(woven, slots, ACT.Copy, scale=gb_high[:, t - 2 : t - 1])

        z_rows = tile([P, PACK, S], BF16, "z_rows")
        for t in range(PACK):
            nc.vector.scalar_tensor_tensor(z_rows[:, t, :], a_acc[t][:], ga_16th[:, t : t + 1], inv_den[:, t, :], MULT, MULT)
        z_in = tile([P, S, PACK], BF16, "z_in")
        nc.scalar.copy(
            z_in[:].rearrange("p (u m) t -> p m t u", u=PACK), z_rows[:].rearrange("p t (m u) -> p m t u", u=PACK)
        )
        zw = tile([P, S], U32, "zw")
        zs = tile([P, S], U8, "zs")
        nc.vector.quantize_mx(out=zw[:].bitcast(FP8X4), scales=zs[:], in_=z_in[:].rearrange("p j t -> p (j t)"))
        z2w = tile([P, U], U32, "z2w")
        z2s = tile([P, U], U8, "z2s")
        z2_in = [tile([P, BANK * PACK], BF16, "z2_in%d" % h) for h in range(U // BANK)]
        for h in range(U // BANK):
            nc.vector.tensor_copy(
                z2_in[h][:].bitcast(I32).rearrange("p (c i e) -> p c e i", i=4, e=2),
                z2_pairs[h][:].rearrange("p e w d -> p e (w d)").bitcast(I32).rearrange("p e (c i) -> p c e i", i=4),
            )
        for h in range(U // BANK):
            cols = slice(h * BANK, (h + 1) * BANK)
            nc.vector.quantize_mx(out=z2w[:, cols].bitcast(FP8X4), scales=z2s[:, cols], in_=z2_in[h][:])

        s_win = [tile([P, U], F32, "s_win%d" % t) for t in range(PACK)]
        s_own = [tile([P, U], F32, "s_own%d" % t) for t in range(PACK)]
        st_win = [tile([P, U], F32, "st_win%d" % t) for t in range(PACK)]
        st_own = [tile([P, U], F32, "st_own%d" % t) for t in range(PACK)]
        for t in range(PACK):
            accs = []
            for h in range(U // BANK):
                cols = slice(h * BANK, (h + 1) * BANK)
                acc = bank(2 * t + h)
                nc.tensor.matmul_mx(
                    acc[:],
                    lhsT=zw[:, P * t : P * (t + 1)].bitcast(FP8X4),
                    lhsT_scale=zs[:, P * t : P * (t + 1)],
                    rhs=z2w[:, cols].bitcast(FP8X4),
                    rhs_scale=z2s[:, cols],
                    start=True,
                    stop=True,
                )
                nc.scalar.activation(s_win[t][:, cols], acc[:], ACT.Copy, scale=0.03125)
                accs.append(acc)
            for h in range(U // BANK):
                cols = slice(h * BANK, (h + 1) * BANK)
                if t == 0:
                    nc.vector.tensor_scalar(s_own[t][:, cols], accs[h][:], 0.03125, None, MULT)
                else:
                    nc.scalar.activation(s_own[t][:, cols], accs[h][:], ACT.Copy, scale=0.03125)
            for h in range(U // BANK):
                cols = slice(h * BANK, (h + 1) * BANK)
                nc.vector.tensor_tensor(st_win[t][:, cols], s_win[t][:].indirect(entries(n3_l, h * BANK, BANK)), s_own[t][:, cols], SUB)
        for first in range(0, U, CHUNK):
            for t in range(PACK):
                cols = slice(first, first + CHUNK)
                nc.scalar.activation(st_own[t][:, cols], st_win[t][:, cols], ACT.Copy, scale=2.0)

        yw = tile([P, U], U32, "yw")
        ys = tile([P, U], U8, "ys")
        out_rows = out_0.rearrange("(p t) w -> p t w", t=PACK)
        out_words = out_1[0].rearrange("p n t -> p (n t)").bitcast(I32)
        for i in range(U // CHUNK):
            first = i * CHUNK
            cols = slice(first, first + CHUNK)
            y = tile([P, PACK, CHUNK], F32, "y%d" % i, "y_in%d" % (i - 2) if i >= 2 else None)
            y_in = tile([P, CHUNK, PACK], BF16, "y_in%d" % i)
            for t in range(PACK):
                nc.vector.tensor_tensor(y[:, t, :], st_win[t][:].indirect(entries(n3_l, first, CHUNK)), st_own[t][:, cols], SUB)
            nc.sync.dma_start(out_rows[:, :, cols], y[:])
            woven = y_in[:].rearrange("p (c i) t -> p c t i", i=4)
            rows = y[:].rearrange("p t (c i) -> p c t i", i=4)
            if i == U // CHUNK - 1:
                nc.vector.tensor_copy(woven, rows)
            else:
                nc.scalar.copy(woven, rows)
            nc.vector.quantize_mx(out=yw[:, cols].bitcast(FP8X4), scales=ys[:, cols], in_=y_in[:].rearrange("p w t -> p (w t)"))
            nc.sync.dma_start(out_words[:, cols], yw[:, cols].bitcast(I32))
        for q in range(4):
            nc.scalar.dma_start(out_2[0][4 * q : 4 * q + 4, :].bitcast(I32), ys[32 * q : 32 * q + 4, :].bitcast(I32))
